import numpy as np
import ml_dtypes


def mxq(x, axis, fmt="e4m3"):
    dtype, down = {"e4m3": (ml_dtypes.float8_e4m3fn, 7), "e5m2": (ml_dtypes.float8_e5m2, 14)}[fmt]
    v = np.moveaxis(np.asarray(x, np.float32).astype(ml_dtypes.bfloat16).astype(np.float64), axis, -1)
    blocks = v.reshape(v.shape[:-1] + (-1, 32))
    amax = np.abs(blocks).max(-1, keepdims=True)
    byte = np.maximum(np.where(amax > 0, np.frexp(amax)[1] - 1 + 127, 0) - down, 1)
    scale = np.exp2(byte - 127.0)
    codes = (blocks / scale).astype(np.float32).astype(dtype).astype(np.float64)
    return np.moveaxis((codes * scale).reshape(v.shape), -1, axis)


WIDE = False


def mx_kscale(k):
    if not WIDE:
        return np.ones(k)
    levels = np.array([30, -30])
    if k % 512:
        return np.exp2(np.random.permutation(np.resize(levels, k // 32))).repeat(32)
    a = np.empty((k // 512, 16))
    for p in range(k // 512):
        a[p, :8] = np.random.permutation(np.resize(levels, 8))
        for g in range(8):
            far = levels[np.abs(levels - a[p, g]) >= 10]
            a[p, g + 8] = far[np.random.randint(len(far))]
    return np.exp2(a.ravel()).repeat(32)


def f64(x):
    return np.asarray(x).astype(np.float64)


def striped(idx):
    return np.tile(np.asarray(idx).reshape(-1, 16).T, (8, 1)).astype(np.uint16)


def unstriped(offs):
    return offs[:16].T.reshape(-1).astype(np.int64)


E2M1 = np.array([0.0, 0.5, 1.0, 1.5, 2.0, 3.0, 4.0, 6.0, -0.0, -0.5, -1.0, -1.5, -2.0, -3.0, -4.0, -6.0])


def pack_weight(w, fmt):
    k, n = w.shape
    w = f64(np.asarray(w, np.float32).astype(ml_dtypes.bfloat16)).reshape(k // 32, 32, n)
    amax = np.abs(w).max(1)
    if fmt == "e4m3":
        byte = np.frexp(amax)[1] - 1 + 127 - 7
    else:
        mant, ex = np.frexp(amax / 6.0)
        byte = np.where(mant > 0.5, ex, ex - 1) + 127
    byte = np.clip(np.where(amax > 0, byte, 1), 1, 254)
    scaled = (w * np.exp2(127.0 - byte)[:, None, :]).reshape(k, n).astype(np.float32)
    by_word = np.ascontiguousarray(scaled.reshape(k // 512, 128, 4, n).transpose(0, 1, 3, 2))
    if fmt == "e4m3":
        words = by_word.astype(ml_dtypes.float8_e4m3fn).view(np.uint8)
    else:
        c = by_word.astype(ml_dtypes.float4_e2m1fn).view(np.uint8) & 0xF
        words = (c[..., 0::2] | (c[..., 1::2] << 4)).reshape(k // 512, 128, 2 * n)
    return np.ascontiguousarray(words), np.ascontiguousarray(byte.astype(np.uint8).reshape(k // 512, 16, n))


def unpack_weight(words, scales, fmt):
    g, _, n = scales.shape
    words = np.ascontiguousarray(words).reshape(g, 128, n, -1)
    if fmt == "e4m3":
        vals = words.view(ml_dtypes.float8_e4m3fn).astype(np.float64)
    else:
        nib = np.empty((g, 128, n, 4), np.uint8)
        nib[..., 0::2] = words & 0xF
        nib[..., 1::2] = words >> 4
        vals = E2M1[nib]
    vals = vals * np.repeat(np.exp2(scales.astype(np.float64) - 127.0), 8, axis=1)[..., None]
    return vals.transpose(0, 1, 3, 2).reshape(g * 512, n)


def bf(x):
    return np.asarray(x, np.float32).astype(ml_dtypes.bfloat16)


def planes(Y):
    r, m = Y.shape
    b = f64(bf(Y)).reshape(r // 32, 32, m)
    amax = np.abs(b).max(1)
    byte = np.clip(np.where(amax > 0, np.frexp(amax)[1] - 1 + 127 - 7, 1), 1, 254)
    codes = (b * np.exp2(127.0 - byte)[:, None, :]).reshape(r, m).astype(np.float32).astype(ml_dtypes.float8_e4m3fn).view(np.uint8)
    words = codes.reshape(r // 512, 128, 4, m).transpose(0, 1, 3, 2)
    return np.ascontiguousarray(words), np.ascontiguousarray(byte.astype(np.uint8).reshape(r // 512, 16, m))


K, R, N, T, J = 512, 512, 512, 1024, 512


def setup_inputs():
    n = np.random.standard_normal
    idx = np.random.permutation(T)[:J]
    fn = mx_kscale(N)
    fr = mx_kscale(R)
    wdp = pack_weight(n((N, R)) * 1 / np.sqrt(N) * fn[:, None], "e4m3")
    wup = pack_weight(n((R, K)) * 1 / np.sqrt(R) / fr[:, None], "e2m1")
    return {
        "g": (n((N, T)) * np.exp(0.5 * n((1, T))) / fn[:, None]).astype(np.float32),
        "wd_words": wdp[0],
        "wd_scales": wdp[1],
        "z": (n((R, T)) * fr[:, None]).astype(np.float32),
        "wu_words": wup[0],
        "wu_scales": wup[1],
        "run": (1.0 * n((K, T))).astype(np.float32),
        "offs": striped(idx),
    }


def reference(g, wd_words, wd_scales, z, wu_words, wu_scales, run, offs):
    idx = unstriped(offs)
    wdu = unpack_weight(wd_words, wd_scales, "e4m3")
    wuu = unpack_weight(wu_words, wu_scales, "e2m1")
    gidxq = mxq(f64(g)[:, idx], 0, "e5m2")
    dh = wdu.T @ gidxq
    dz = 2.0 * dh * np.maximum(f64(z)[:, idx], 0.0)
    dzq = mxq(dz, 0, "e5m2")
    dx = wuu.T @ dzq
    p = np.zeros((K, T))
    p[:, idx] = dx
    y = p + 0.3 * f64(run)
    words, scales = planes(y)
    return y, words, scales

@@ -1,0 +1,185 @@
+from contextlib import ExitStack
+
+import concourse.mybir as mybir
+
+F32 = mybir.dt.float32
+BF16 = mybir.dt.bfloat16
+I32 = mybir.dt.int32
+U32 = mybir.dt.uint32
+U16 = mybir.dt.uint16
+U8 = mybir.dt.uint8
+E4M3 = mybir.dt.float8_e4m3fn_x4
+E5M2 = mybir.dt.float8_e5m2_x4
+E2M1 = mybir.dt.float4_e2m1fn_x4
+ALU = mybir.AluOpType
+COPY = mybir.ActivationFunctionType.Copy
+
+P = 128
+PACK = 4
+D = 512
+T = 1024
+J = 512
+CHUNK = 256
+CHUNKS = T // CHUNK
+DZ_VECTOR_COLS = 352
+RUN_SHARE = 0.3
+
+FLOPS = 2 * 2 * D * D * J
+
+
+def tile_list_squared_relu_back_pl_kernel(tc, g, wd_words, wd_scales, z, wu_words, wu_scales, run, offs, out_0, out_1, out_2):
+    nc = tc.nc
+    with ExitStack() as ctx:
+        sb = ctx.enter_context(tc.tile_pool(name="sb", bufs=1))
+        ps = ctx.enter_context(tc.psum_pool(name="ps", bufs=1))
+
+        def tile(name, shape, dtype, tag=None):
+            return sb.tile(shape, dtype, name=name, tag=tag or name, align_bytes=64)
+
+        def dealt_rows(x, t):
+            return x.rearrange("(p t) c -> p t c", t=PACK)[:, t, :]
+
+        def load_planes(name, x, planes):
+            tiles = []
+            for t in planes:
+                plane = tile("%s%d" % (name, t), [P, T], F32)
+                nc.sync.dma_start(out=plane[:], in_=dealt_rows(x, t))
+                tiles.append(plane)
+            return tiles
+
+        def load_scale_rows(raw, scales):
+            rows = scales[0].bitcast(I32)
+            for q in range(4):
+                nc.sync.dma_start(out=raw[32 * q : 32 * q + 4, :].bitcast(I32), in_=rows[4 * q : 4 * q + 4, :])
+
+        def deal_scales(name, raw):
+            dealt = tile(name, [P, D], U8)
+            nc.gpsimd.tensor_copy(out=dealt[:].rearrange("p (t m) -> p t m", t=PACK), in_=raw[:].rearrange("p (m t) -> p t m", t=PACK))
+            return dealt
+
+        offsets = sb.tile([P, J // 16], U16, name="offsets")
+        nc.sync.dma_start(offsets[:], offs)
+
+        wd_scale_raw = tile("wd_scale_raw", [P, D], U8)
+        wu_scale_raw = tile("wu_scale_raw", [P, D], U8)
+        nc.gpsimd.memset(wd_scale_raw[:].bitcast(U32), 0)
+        nc.gpsimd.memset(wu_scale_raw[:].bitcast(U32), 0)
+        pages = []
+        for t in range(PACK):
+            page = tile("page%d" % t, [P, T], F32)
+            nc.gpsimd.memset(page[:], 0.0)
+            pages.append(page)
+
+        g_planes = load_planes("g", g, range(PACK))
+        load_scale_rows(wd_scale_raw, wd_scales)
+        z_planes = load_planes("z", z, range(1))
+        wd_raw = tile("wd_raw", [P, D], U32)
+        nc.sync.dma_start(out=wd_raw[:].bitcast(I32), in_=wd_words[0].rearrange("p c t -> p (c t)").bitcast(I32))
+        z_planes.extend(load_planes("z", z, range(1, PACK)))
+        load_scale_rows(wu_scale_raw, wu_scales)
+        wu_raw = tile("wu_raw", [P, 2 * D], U8)
+        nc.sync.dma_start(out=wu_raw[:].bitcast(I32), in_=wu_words[0].bitcast(I32))
+        run_planes = load_planes("run", run, range(PACK))
+
+        wd_scale = deal_scales("wd_scale", wd_scale_raw)
+        wd = tile("wd", [P, D], U32)
+        nc.gpsimd.tensor_copy(out=wd[:].rearrange("p (t m) -> p t m", t=PACK), in_=wd_raw[:].rearrange("p (m t) -> p t m", t=PACK))
+        wu_scale = deal_scales("wu_scale", wu_scale_raw)
+        wu = tile("wu", [P, 2 * D], U8)
+        nc.gpsimd.tensor_copy(
+            out=wu[:].rearrange("p (t m b) -> p t m b", t=PACK, b=2), in_=wu_raw[:].rearrange("p (m t b) -> p t m b", t=PACK, b=2)
+        )
+
+        g_woven = tile("g_woven", [P, J, PACK], BF16)
+        for pair in range(2):
+            picked = tile("g_picked%d" % pair, [P, 2, J], F32)
+            for e in range(2):
+                nc.vector.tensor_copy(out=picked[:, e, :], in_=g_planes[2 * pair + e][:].indirect(offsets[:]))
+            nc.scalar.copy(out=g_woven[:, :, 2 * pair : 2 * pair + 2], in_=picked[:].rearrange("p e j -> p j e"))
+
+        z_picked = []
+        for t in range(PACK):
+            picked = tile("z_picked%d" % t, [P, J], F32)
+            nc.vector.tensor_copy(out=picked[:], in_=z_planes[t][:].indirect(offsets[:]))
+            z_picked.append(picked)
+
+        g_codes = tile("g_codes", [P, J], U32, tag="z1")
+        g_scale = tile("g_scale", [P, J], U8)
+        nc.vector.quantize_mx(out=g_codes[:].bitcast(E5M2), scales=g_scale[:], in_=g_woven[:].rearrange("p j t -> p (j t)"))
+
+        half_dz = tile("half_dz", [P, PACK, J], F32)
+        for t in range(PACK):
+            dh = ps.tile([P, J], F32, name="dh%d" % t)
+            cols = slice(P * t, P * (t + 1))
+            nc.tensor.matmul_mx(
+                out=dh[:], lhsT=wd[:, cols].bitcast(E4M3), lhsT_scale=wd_scale[:, cols],
+                rhs=g_codes[:].bitcast(E5M2), rhs_scale=g_scale[:], start=True, stop=True,
+            )
+            nc.vector.scalar_tensor_tensor(
+                out=half_dz[:, t, :], in0=z_picked[t][:], scalar=0.0, in1=dh[:], op0=ALU.max, op1=ALU.mult
+            )
+
+        share0 = tile("share0", [P, T], F32)
+        nc.scalar.activation(out=share0[:], in_=run_planes[0][:], func=COPY, scale=RUN_SHARE)
+
+        dz_woven = tile("dz_woven", [P, J, PACK], BF16)
+        woven = dz_woven[:].rearrange("p (c i) t -> p c t i", i=4)
+        planes = half_dz[:].rearrange("p t (c i) -> p c t i", i=4)
+        split = DZ_VECTOR_COLS // 4
+        nc.vector.tensor_scalar(out=woven[:, :split], in0=planes[:, :split], scalar1=2.0, scalar2=None, op0=ALU.mult)
+        nc.scalar.activation(out=woven[:, split:], in_=planes[:, split:], func=COPY, scale=2.0)
+        dz_codes = tile("dz_codes", [P, J], U32)
+        dz_scale = tile("dz_scale", [P, J], U8)
+        nc.vector.quantize_mx(out=dz_codes[:].bitcast(E5M2), scales=dz_scale[:], in_=dz_woven[:].rearrange("p j t -> p (j t)"))
+
+        for t in range(PACK):
+            dx = ps.tile([P, J], F32, name="dx%d" % t)
+            nc.tensor.matmul_mx(
+                out=dx[:], lhsT=wu[:, 2 * P * t : 2 * P * (t + 1)].bitcast(E2M1), lhsT_scale=wu_scale[:, P * t : P * (t + 1)],
+                rhs=dz_codes[:].bitcast(E5M2), rhs_scale=dz_scale[:], start=True, stop=True,
+            )
+            dx_sb = tile("dx_sb%d" % t, [P, J], F32)
+            nc.scalar.copy(out=dx_sb[:], in_=dx[:])
+            nc.vector.tensor_copy(out=pages[t][:].indirect(offsets[:]), in_=dx_sb[:])
+
+        share1 = tile("share1", [P, T], F32, tag="dz_codes")
+        nc.scalar.activation(out=share1[:], in_=run_planes[1][:], func=COPY, scale=RUN_SHARE)
+        y23 = tile("y23", [P, 2, T], F32, tag="wu")
+        nc.scalar.activation(out=y23[:, 1, :], in_=run_planes[2][:], func=COPY, scale=RUN_SHARE)
+
+        y01 = tile("y01", [P, 2, T], F32)
+        for t, share in enumerate((share0, share1)):
+            nc.gpsimd.tensor_tensor(out=y01[:, t, :], in0=pages[t][:], in1=share[:], op=ALU.add)
+            nc.sync.dma_start(out=dealt_rows(out_0, t), in_=y01[:, t, :])
+        nc.gpsimd.tensor_tensor(out=y23[:, 0, :], in0=pages[2][:], in1=y23[:, 1, :], op=ALU.add)
+        nc.sync.dma_start(out=dealt_rows(out_0, 2), in_=y23[:, 0, :])
+
+        y_woven = [tile("y_woven%d" % c, [P, CHUNK, PACK], BF16) for c in range(CHUNKS)]
+        chunk_cols = [slice(CHUNK * c, CHUNK * (c + 1)) for c in range(CHUNKS)]
+        for c, cols in enumerate(chunk_cols):
+            nc.scalar.copy(out=y_woven[c][:, :, 0:2], in_=y01[:, :, cols].rearrange("p e c -> p c e"))
+        for c, cols in enumerate(chunk_cols):
+            nc.vector.scalar_tensor_tensor(
+                out=y23[:, 1, cols], in0=run_planes[3][:, cols], scalar=RUN_SHARE, in1=pages[3][:, cols], op0=ALU.mult, op1=ALU.add
+            )
+            if c % 2:
+                half = slice(CHUNK * (c - 1), CHUNK * (c + 1))
+                nc.sync.dma_start(out=dealt_rows(out_0, 3)[:, half], in_=y23[:, 1, half])
+        for c, cols in enumerate(chunk_cols):
+            src = y23[:, :, cols].rearrange("p e c -> p c e")
+            if c < CHUNKS // 2:
+                nc.scalar.copy(out=y_woven[c][:, :, 2:4], in_=src)
+            else:
+                nc.vector.tensor_copy(out=y_woven[c][:, :, 2:4], in_=src)
+        y_scale = tile("y_scale", [P, T], U8)
+        words = out_1[0].rearrange("p c t -> p (c t)").bitcast(I32)
+        for c in (2, 0, 3, 1):
+            y_codes = tile("y_codes%d" % c, [P, CHUNK], U32)
+            nc.vector.quantize_mx(
+                out=y_codes[:].bitcast(E4M3), scales=y_scale[:, chunk_cols[c]], in_=y_woven[c][:].rearrange("p c t -> p (c t)")
+            )
+            nc.sync.dma_start(out=words[:, chunk_cols[c]], in_=y_codes[:].bitcast(I32))
+        scale_rows = out_2[0].bitcast(I32)
+        for q in range(4):
+            queue = nc.sync if q % 2 else nc.scalar
+            queue.dma_start(out=scale_rows[4 * q : 4 * q + 4, :], in_=y_scale[32 * q : 32 * q + 4, :].bitcast(I32))

@@ -21,7 +21,7 @@ T = 1024
 J = 512
 CHUNK = 256
 CHUNKS = T // CHUNK
-DZ_VECTOR_COLS = 352
+HALF = J // 2
 RUN_SHARE = 0.3
 
 FLOPS = 2 * 2 * D * D * J
@@ -57,9 +57,6 @@ def tile_list_squared_relu_back_pl_kernel(tc, g, wd_words, wd_scales, z, wu_word
             nc.gpsimd.tensor_copy(out=dealt[:].rearrange("p (t m) -> p t m", t=PACK), in_=raw[:].rearrange("p (m t) -> p t m", t=PACK))
             return dealt
 
-        offsets = sb.tile([P, J // 16], U16, name="offsets")
-        nc.sync.dma_start(offsets[:], offs)
-
         wd_scale_raw = tile("wd_scale_raw", [P, D], U8)
         wu_scale_raw = tile("wu_scale_raw", [P, D], U8)
         nc.gpsimd.memset(wd_scale_raw[:].bitcast(U32), 0)
@@ -70,7 +67,10 @@ def tile_list_squared_relu_back_pl_kernel(tc, g, wd_words, wd_scales, z, wu_word
             nc.gpsimd.memset(page[:], 0.0)
             pages.append(page)
 
-        g_planes = load_planes("g", g, range(PACK))
+        g_planes = load_planes("g", g, range(1))
+        offsets = sb.tile([P, J // 16], U16, name="offsets")
+        nc.sync.dma_start(offsets[:], offs)
+        g_planes.extend(load_planes("g", g, range(1, PACK)))
         load_scale_rows(wd_scale_raw, wd_scales)
         z_planes = load_planes("z", z, range(1))
         wd_raw = tile("wd_raw", [P, D], U32)
@@ -84,96 +84,136 @@ def tile_list_squared_relu_back_pl_kernel(tc, g, wd_words, wd_scales, z, wu_word
         wd_scale = deal_scales("wd_scale", wd_scale_raw)
         wd = tile("wd", [P, D], U32)
         nc.gpsimd.tensor_copy(out=wd[:].rearrange("p (t m) -> p t m", t=PACK), in_=wd_raw[:].rearrange("p (m t) -> p t m", t=PACK))
-        wu_scale = deal_scales("wu_scale", wu_scale_raw)
-        wu = tile("wu", [P, 2 * D], U8)
-        nc.gpsimd.tensor_copy(
-            out=wu[:].rearrange("p (t m b) -> p t m b", t=PACK, b=2), in_=wu_raw[:].rearrange("p (m t b) -> p t m b", t=PACK, b=2)
-        )
+
+        def deal_wu(engine, name, slices, tags):
+            count = slices.stop - slices.start
+            scale = tile(name + "_scale", [P, count, P], U8, tag=tags[0])
+            engine.tensor_copy(out=scale[:], in_=wu_scale_raw[:].rearrange("p (m t) -> p t m", t=PACK)[:, slices])
+            codes = tile(name, [P, count, P, 2], U8, tag=tags[1])
+            engine.tensor_copy(out=codes[:], in_=wu_raw[:].rearrange("p (m t b) -> p t m b", t=PACK, b=2)[:, slices])
+            return [(codes[:, i].rearrange("p m b -> p (m b)"), scale[:, i, :]) for i in range(count)]
+
+        wu = deal_wu(nc.gpsimd, "wu_first", slice(0, 1), (None, None))
 
         g_woven = tile("g_woven", [P, J, PACK], BF16)
         for pair in range(2):
             picked = tile("g_picked%d" % pair, [P, 2, J], F32)
             for e in range(2):
                 nc.vector.tensor_copy(out=picked[:, e, :], in_=g_planes[2 * pair + e][:].indirect(offsets[:]))
-            nc.scalar.copy(out=g_woven[:, :, 2 * pair : 2 * pair + 2], in_=picked[:].rearrange("p e j -> p j e"))
+            nc.scalar.activation(out=g_woven[:, :, 2 * pair : 2 * pair + 2], in_=picked[:].rearrange("p e j -> p j e"), func=COPY)
 
         z_picked = []
-        for t in range(PACK):
+        for t in range(PACK - 1):
             picked = tile("z_picked%d" % t, [P, J], F32)
             nc.vector.tensor_copy(out=picked[:], in_=z_planes[t][:].indirect(offsets[:]))
             z_picked.append(picked)
+        z_last = []
+        for h in range(2):
+            picked = tile("z_last%d" % h, [P, HALF], F32)
+            nc.vector.tensor_copy(out=picked[:], in_=z_planes[PACK - 1][:].indirect(offsets[:, 16 * h : 16 * (h + 1)]))
+            z_last.append(picked)
 
         g_codes = tile("g_codes", [P, J], U32, tag="z1")
         g_scale = tile("g_scale", [P, J], U8)
         nc.vector.quantize_mx(out=g_codes[:].bitcast(E5M2), scales=g_scale[:], in_=g_woven[:].rearrange("p j t -> p (j t)"))
 
-        half_dz = tile("half_dz", [P, PACK, J], F32)
+        dh = []
         for t in range(PACK):
-            dh = ps.tile([P, J], F32, name="dh%d" % t)
+            bank = ps.tile([P, J], F32, name="dh%d" % t)
             cols = slice(P * t, P * (t + 1))
             nc.tensor.matmul_mx(
-                out=dh[:], lhsT=wd[:, cols].bitcast(E4M3), lhsT_scale=wd_scale[:, cols],
+                out=bank[:], lhsT=wd[:, cols].bitcast(E4M3), lhsT_scale=wd_scale[:, cols],
                 rhs=g_codes[:].bitcast(E5M2), rhs_scale=g_scale[:], start=True, stop=True,
             )
-            nc.vector.scalar_tensor_tensor(
-                out=half_dz[:, t, :], in0=z_picked[t][:], scalar=0.0, in1=dh[:], op0=ALU.max, op1=ALU.mult
+            dh.append(bank)
+
+        def half_product(out, picked, bank):
+            nc.vector.scalar_tensor_tensor(out=out, in0=picked, scalar=0.0, in1=bank, op0=ALU.max, op1=ALU.mult)
+
+        def by_halves(x):
+            return x.rearrange("p (h j) -> p h j", h=2)
+
+        dz_woven = [tile("dz_woven%d" % h, [P, HALF, PACK], BF16) for h in range(2)]
+        product01 = tile("product01", [P, 2, J], F32)
+        for t in range(2):
+            half_product(product01[:, t, :], z_picked[t][:], dh[t][:])
+        for h in range(2):
+            nc.scalar.activation(
+                out=dz_woven[h][:, :, 0:2], in_=product01[:, :, HALF * h : HALF * (h + 1)].rearrange("p e j -> p j e"), func=COPY, scale=2.0
             )
-
-        share0 = tile("share0", [P, T], F32)
-        nc.scalar.activation(out=share0[:], in_=run_planes[0][:], func=COPY, scale=RUN_SHARE)
-
-        dz_woven = tile("dz_woven", [P, J, PACK], BF16)
-        woven = dz_woven[:].rearrange("p (c i) t -> p c t i", i=4)
-        planes = half_dz[:].rearrange("p t (c i) -> p c t i", i=4)
-        split = DZ_VECTOR_COLS // 4
-        nc.vector.tensor_scalar(out=woven[:, :split], in0=planes[:, :split], scalar1=2.0, scalar2=None, op0=ALU.mult)
-        nc.scalar.activation(out=woven[:, split:], in_=planes[:, split:], func=COPY, scale=2.0)
+        product23 = tile("product23", [P, 2, 2, HALF], F32)
+        half_product(product23[:, :, 0, :], by_halves(z_picked[2][:]), by_halves(dh[2][:]))
+        for h in range(2):
+            half_product(product23[:, h, 1, :], z_last[h][:], dh[3][:, HALF * h : HALF * (h + 1)])
+        nc.scalar.activation(out=dz_woven[0][:, :, 2:4], in_=product23[:, 0].rearrange("p e j -> p j e"), func=COPY, scale=2.0)
+        nc.vector.tensor_scalar(
+            out=dz_woven[1][:, :, 2:4], in0=product23[:, 1].rearrange("p e j -> p j e"), scalar1=2.0, scalar2=None, op0=ALU.mult
+        )
         dz_codes = tile("dz_codes", [P, J], U32)
         dz_scale = tile("dz_scale", [P, J], U8)
-        nc.vector.quantize_mx(out=dz_codes[:].bitcast(E5M2), scales=dz_scale[:], in_=dz_woven[:].rearrange("p j t -> p (j t)"))
+        for h in range(2):
+            cols = slice(HALF * h, HALF * (h + 1))
+            nc.vector.quantize_mx(
+                out=dz_codes[:, cols].bitcast(E5M2), scales=dz_scale[:, cols], in_=dz_woven[h][:].rearrange("p j t -> p (j t)")
+            )
 
+        wu.extend(deal_wu(nc.vector, "wu_rest", slice(1, PACK), ("dz_woven0", "dz_woven1")))
         for t in range(PACK):
             dx = ps.tile([P, J], F32, name="dx%d" % t)
             nc.tensor.matmul_mx(
-                out=dx[:], lhsT=wu[:, 2 * P * t : 2 * P * (t + 1)].bitcast(E2M1), lhsT_scale=wu_scale[:, P * t : P * (t + 1)],
+                out=dx[:], lhsT=wu[t][0].bitcast(E2M1), lhsT_scale=wu[t][1],
                 rhs=dz_codes[:].bitcast(E5M2), rhs_scale=dz_scale[:], start=True, stop=True,
             )
             dx_sb = tile("dx_sb%d" % t, [P, J], F32)
             nc.scalar.copy(out=dx_sb[:], in_=dx[:])
             nc.vector.tensor_copy(out=pages[t][:].indirect(offsets[:]), in_=dx_sb[:])
 
+        share0 = tile("share0", [P, T], F32)
+        nc.scalar.activation(out=share0[:], in_=run_planes[0][:], func=COPY, scale=RUN_SHARE)
         share1 = tile("share1", [P, T], F32, tag="dz_codes")
         nc.scalar.activation(out=share1[:], in_=run_planes[1][:], func=COPY, scale=RUN_SHARE)
-        y23 = tile("y23", [P, 2, T], F32, tag="wu")
-        nc.scalar.activation(out=y23[:, 1, :], in_=run_planes[2][:], func=COPY, scale=RUN_SHARE)
+        y23 = tile("y23", [P, CHUNKS, 2, CHUNK], F32, tag="dz_woven1")
 
-        y01 = tile("y01", [P, 2, T], F32)
-        for t, share in enumerate((share0, share1)):
-            nc.gpsimd.tensor_tensor(out=y01[:, t, :], in0=pages[t][:], in1=share[:], op=ALU.add)
-            nc.sync.dma_start(out=dealt_rows(out_0, t), in_=y01[:, t, :])
-        nc.gpsimd.tensor_tensor(out=y23[:, 0, :], in0=pages[2][:], in1=y23[:, 1, :], op=ALU.add)
-        nc.sync.dma_start(out=dealt_rows(out_0, 2), in_=y23[:, 0, :])
+        def by_chunks(x):
+            return x.rearrange("p (c i) -> p c i", i=CHUNK)
+
+        nc.scalar.activation(out=y23[:, :, 1, :], in_=by_chunks(run_planes[2][:]), func=COPY, scale=RUN_SHARE)
+
+        y01 = tile("y01", [P, 2, 2, T // 2], F32)
+        nc.gpsimd.tensor_tensor(
+            out=y01[:, :, 0, :], in0=pages[0][:].rearrange("p (h i) -> p h i", h=2), in1=share0[:].rearrange("p (h i) -> p h i", h=2), op=ALU.add
+        )
+        nc.sync.dma_start(out=dealt_rows(out_0, 0).rearrange("p (h i) -> p h i", h=2), in_=y01[:, :, 0, :])
+        for h in range(2):
+            cols = slice(T // 2 * h, T // 2 * (h + 1))
+            nc.gpsimd.tensor_tensor(out=y01[:, h, 1, :], in0=pages[1][:, cols], in1=share1[:, cols], op=ALU.add)
+        nc.sync.dma_start(out=dealt_rows(out_0, 1).rearrange("p (h i) -> p h i", h=2), in_=y01[:, :, 1, :])
+        nc.gpsimd.tensor_tensor(out=y23[:, :, 0, :], in0=by_chunks(pages[2][:]), in1=y23[:, :, 1, :], op=ALU.add)
+        nc.sync.dma_start(out=by_chunks(dealt_rows(out_0, 2)), in_=y23[:, :, 0, :])
 
         y_woven = [tile("y_woven%d" % c, [P, CHUNK, PACK], BF16) for c in range(CHUNKS)]
         chunk_cols = [slice(CHUNK * c, CHUNK * (c + 1)) for c in range(CHUNKS)]
-        for c, cols in enumerate(chunk_cols):
-            nc.scalar.copy(out=y_woven[c][:, :, 0:2], in_=y01[:, :, cols].rearrange("p e c -> p c e"))
-        for c, cols in enumerate(chunk_cols):
+        for c in range(CHUNKS):
+            cols = slice(CHUNK * (c % 2), CHUNK * (c % 2 + 1))
+            nc.scalar.copy(out=y_woven[c][:, :, 0:2], in_=y01[:, c // 2, :, cols].rearrange("p e c -> p c e"))
+        for chunks in (slice(0, 1), slice(1, 2), slice(2, 4)):
             nc.vector.scalar_tensor_tensor(
-                out=y23[:, 1, cols], in0=run_planes[3][:, cols], scalar=RUN_SHARE, in1=pages[3][:, cols], op0=ALU.mult, op1=ALU.add
+                out=y23[:, chunks, 1, :], in0=by_chunks(run_planes[3][:])[:, chunks], scalar=RUN_SHARE,
+                in1=by_chunks(pages[3][:])[:, chunks], op0=ALU.mult, op1=ALU.add,
             )
-            if c % 2:
-                half = slice(CHUNK * (c - 1), CHUNK * (c + 1))
-                nc.sync.dma_start(out=dealt_rows(out_0, 3)[:, half], in_=y23[:, 1, half])
-        for c, cols in enumerate(chunk_cols):
-            src = y23[:, :, cols].rearrange("p e c -> p c e")
-            if c < CHUNKS // 2:
-                nc.scalar.copy(out=y_woven[c][:, :, 2:4], in_=src)
-            else:
-                nc.vector.tensor_copy(out=y_woven[c][:, :, 2:4], in_=src)
+        for chunks in (slice(0, 2), slice(2, 4)):
+            nc.sync.dma_start(out=by_chunks(dealt_rows(out_0, 3))[:, chunks], in_=y23[:, chunks, 1, :])
+        for engine_copy, c, cols in (
+            (nc.scalar.copy, 0, slice(0, CHUNK)),
+            (nc.vector.tensor_copy, 1, slice(0, CHUNK)),
+            (nc.scalar.copy, 2, slice(0, CHUNK)),
+            (nc.vector.tensor_copy, 3, slice(CHUNK // 2, CHUNK)),
+            (nc.scalar.copy, 3, slice(0, CHUNK // 2)),
+        ):
+            engine_copy(out=y_woven[c][:, cols, 2:4], in_=y23[:, c, :, cols].rearrange("p e c -> p c e"))
         y_scale = tile("y_scale", [P, T], U8)
         words = out_1[0].rearrange("p c t -> p (c t)").bitcast(I32)
-        for c in (2, 0, 3, 1):
+        for c in range(CHUNKS):
             y_codes = tile("y_codes%d" % c, [P, CHUNK], U32)
             nc.vector.quantize_mx(
                 out=y_codes[:].bitcast(E4M3), scales=y_scale[:, chunk_cols[c]], in_=y_woven[c][:].rearrange("p c t -> p (c t)")

from contextlib import ExitStack

import concourse.mybir as mybir

F32 = mybir.dt.float32
BF16 = mybir.dt.bfloat16
I32 = mybir.dt.int32
U32 = mybir.dt.uint32
U16 = mybir.dt.uint16
U8 = mybir.dt.uint8
E4M3 = mybir.dt.float8_e4m3fn_x4
E5M2 = mybir.dt.float8_e5m2_x4
E2M1 = mybir.dt.float4_e2m1fn_x4
ALU = mybir.AluOpType
COPY = mybir.ActivationFunctionType.Copy

P = 128
PACK = 4
D = 512
T = 1024
J = 512
CHUNK = 256
CHUNKS = T // CHUNK
HALF = J // 2
RUN_SHARE = 0.3

FLOPS = 2 * 2 * D * D * J


def tile_list_squared_relu_back_pl_kernel(tc, g, wd_words, wd_scales, z, wu_words, wu_scales, run, offs, out_0, out_1, out_2):
    nc = tc.nc
    with ExitStack() as ctx:
        sb = ctx.enter_context(tc.tile_pool(name="sb", bufs=1))
        ps = ctx.enter_context(tc.psum_pool(name="ps", bufs=1))

        def tile(name, shape, dtype, tag=None):
            return sb.tile(shape, dtype, name=name, tag=tag or name, align_bytes=64)

        def dealt_rows(x, t):
            return x.rearrange("(p t) c -> p t c", t=PACK)[:, t, :]

        def load_planes(name, x, planes):
            tiles = []
            for t in planes:
                plane = tile("%s%d" % (name, t), [P, T], F32)
                nc.sync.dma_start(out=plane[:], in_=dealt_rows(x, t))
                tiles.append(plane)
            return tiles

        def load_scale_rows(raw, scales):
            rows = scales[0].bitcast(I32)
            for q in range(4):
                nc.sync.dma_start(out=raw[32 * q : 32 * q + 4, :].bitcast(I32), in_=rows[4 * q : 4 * q + 4, :])

        def deal_scales(name, raw):
            dealt = tile(name, [P, D], U8)
            nc.gpsimd.tensor_copy(out=dealt[:].rearrange("p (t m) -> p t m", t=PACK), in_=raw[:].rearrange("p (m t) -> p t m", t=PACK))
            return dealt

        wd_scale_raw = tile("wd_scale_raw", [P, D], U8)
        wu_scale_raw = tile("wu_scale_raw", [P, D], U8)
        nc.gpsimd.memset(wd_scale_raw[:].bitcast(U32), 0)
        nc.gpsimd.memset(wu_scale_raw[:].bitcast(U32), 0)
        pages = []
        for t in range(PACK):
            page = tile("page%d" % t, [P, T], F32)
            nc.gpsimd.memset(page[:], 0.0)
            pages.append(page)

        g_planes = load_planes("g", g, range(1))
        offsets = sb.tile([P, J // 16], U16, name="offsets")
        nc.sync.dma_start(offsets[:], offs)
        g_planes.extend(load_planes("g", g, range(1, PACK)))
        load_scale_rows(wd_scale_raw, wd_scales)
        z_planes = load_planes("z", z, range(1))
        wd_raw = tile("wd_raw", [P, D], U32)
        nc.sync.dma_start(out=wd_raw[:].bitcast(I32), in_=wd_words[0].rearrange("p c t -> p (c t)").bitcast(I32))
        z_planes.extend(load_planes("z", z, range(1, PACK)))
        load_scale_rows(wu_scale_raw, wu_scales)
        wu_raw = tile("wu_raw", [P, 2 * D], U8)
        nc.sync.dma_start(out=wu_raw[:].bitcast(I32), in_=wu_words[0].bitcast(I32))
        run_planes = load_planes("run", run, range(PACK))

        wd_scale = deal_scales("wd_scale", wd_scale_raw)
        wd = tile("wd", [P, D], U32)
        nc.gpsimd.tensor_copy(out=wd[:].rearrange("p (t m) -> p t m", t=PACK), in_=wd_raw[:].rearrange("p (m t) -> p t m", t=PACK))

        def deal_wu(engine, name, slices, tags):
            count = slices.stop - slices.start
            scale = tile(name + "_scale", [P, count, P], U8, tag=tags[0])
            engine.tensor_copy(out=scale[:], in_=wu_scale_raw[:].rearrange("p (m t) -> p t m", t=PACK)[:, slices])
            codes = tile(name, [P, count, P, 2], U8, tag=tags[1])
            engine.tensor_copy(out=codes[:], in_=wu_raw[:].rearrange("p (m t b) -> p t m b", t=PACK, b=2)[:, slices])
            return [(codes[:, i].rearrange("p m b -> p (m b)"), scale[:, i, :]) for i in range(count)]

        wu = deal_wu(nc.gpsimd, "wu_first", slice(0, 1), (None, None))

        g_woven = tile("g_woven", [P, J, PACK], BF16)
        for pair in range(2):
            picked = tile("g_picked%d" % pair, [P, 2, J], F32)
            for e in range(2):
                nc.vector.tensor_copy(out=picked[:, e, :], in_=g_planes[2 * pair + e][:].indirect(offsets[:]))
            nc.scalar.activation(out=g_woven[:, :, 2 * pair : 2 * pair + 2], in_=picked[:].rearrange("p e j -> p j e"), func=COPY)

        z_picked = []
        for t in range(PACK - 1):
            picked = tile("z_picked%d" % t, [P, J], F32)
            nc.vector.tensor_copy(out=picked[:], in_=z_planes[t][:].indirect(offsets[:]))
            z_picked.append(picked)
        z_last = []
        for h in range(2):
            picked = tile("z_last%d" % h, [P, HALF], F32)
            nc.vector.tensor_copy(out=picked[:], in_=z_planes[PACK - 1][:].indirect(offsets[:, 16 * h : 16 * (h + 1)]))
            z_last.append(picked)

        g_codes = tile("g_codes", [P, J], U32, tag="z1")
        g_scale = tile("g_scale", [P, J], U8)
        nc.vector.quantize_mx(out=g_codes[:].bitcast(E5M2), scales=g_scale[:], in_=g_woven[:].rearrange("p j t -> p (j t)"))

        dh = []
        for t in range(PACK):
            bank = ps.tile([P, J], F32, name="dh%d" % t)
            cols = slice(P * t, P * (t + 1))
            nc.tensor.matmul_mx(
                out=bank[:], lhsT=wd[:, cols].bitcast(E4M3), lhsT_scale=wd_scale[:, cols],
                rhs=g_codes[:].bitcast(E5M2), rhs_scale=g_scale[:], start=True, stop=True,
            )
            dh.append(bank)

        def half_product(out, picked, bank):
            nc.vector.scalar_tensor_tensor(out=out, in0=picked, scalar=0.0, in1=bank, op0=ALU.max, op1=ALU.mult)

        def by_halves(x):
            return x.rearrange("p (h j) -> p h j", h=2)

        dz_woven = [tile("dz_woven%d" % h, [P, HALF, PACK], BF16) for h in range(2)]
        product01 = tile("product01", [P, 2, J], F32)
        for t in range(2):
            half_product(product01[:, t, :], z_picked[t][:], dh[t][:])
        for h in range(2):
            nc.scalar.activation(
                out=dz_woven[h][:, :, 0:2], in_=product01[:, :, HALF * h : HALF * (h + 1)].rearrange("p e j -> p j e"), func=COPY, scale=2.0
            )
        product23 = tile("product23", [P, 2, 2, HALF], F32)
        half_product(product23[:, :, 0, :], by_halves(z_picked[2][:]), by_halves(dh[2][:]))
        for h in range(2):
            half_product(product23[:, h, 1, :], z_last[h][:], dh[3][:, HALF * h : HALF * (h + 1)])
        nc.scalar.activation(out=dz_woven[0][:, :, 2:4], in_=product23[:, 0].rearrange("p e j -> p j e"), func=COPY, scale=2.0)
        nc.vector.tensor_scalar(
            out=dz_woven[1][:, :, 2:4], in0=product23[:, 1].rearrange("p e j -> p j e"), scalar1=2.0, scalar2=None, op0=ALU.mult
        )
        dz_codes = tile("dz_codes", [P, J], U32)
        dz_scale = tile("dz_scale", [P, J], U8)
        for h in range(2):
            cols = slice(HALF * h, HALF * (h + 1))
            nc.vector.quantize_mx(
                out=dz_codes[:, cols].bitcast(E5M2), scales=dz_scale[:, cols], in_=dz_woven[h][:].rearrange("p j t -> p (j t)")
            )

        wu.extend(deal_wu(nc.vector, "wu_rest", slice(1, PACK), ("dz_woven0", "dz_woven1")))
        for t in range(PACK):
            dx = ps.tile([P, J], F32, name="dx%d" % t)
            nc.tensor.matmul_mx(
                out=dx[:], lhsT=wu[t][0].bitcast(E2M1), lhsT_scale=wu[t][1],
                rhs=dz_codes[:].bitcast(E5M2), rhs_scale=dz_scale[:], start=True, stop=True,
            )
            dx_sb = tile("dx_sb%d" % t, [P, J], F32)
            nc.scalar.copy(out=dx_sb[:], in_=dx[:])
            nc.vector.tensor_copy(out=pages[t][:].indirect(offsets[:]), in_=dx_sb[:])

        share0 = tile("share0", [P, T], F32)
        nc.scalar.activation(out=share0[:], in_=run_planes[0][:], func=COPY, scale=RUN_SHARE)
        share1 = tile("share1", [P, T], F32, tag="dz_codes")
        nc.scalar.activation(out=share1[:], in_=run_planes[1][:], func=COPY, scale=RUN_SHARE)
        y23 = tile("y23", [P, CHUNKS, 2, CHUNK], F32, tag="dz_woven1")

        def by_chunks(x):
            return x.rearrange("p (c i) -> p c i", i=CHUNK)

        nc.scalar.activation(out=y23[:, :, 1, :], in_=by_chunks(run_planes[2][:]), func=COPY, scale=RUN_SHARE)

        y01 = tile("y01", [P, 2, 2, T // 2], F32)
        nc.gpsimd.tensor_tensor(
            out=y01[:, :, 0, :], in0=pages[0][:].rearrange("p (h i) -> p h i", h=2), in1=share0[:].rearrange("p (h i) -> p h i", h=2), op=ALU.add
        )
        nc.sync.dma_start(out=dealt_rows(out_0, 0).rearrange("p (h i) -> p h i", h=2), in_=y01[:, :, 0, :])
        for h in range(2):
            cols = slice(T // 2 * h, T // 2 * (h + 1))
            nc.gpsimd.tensor_tensor(out=y01[:, h, 1, :], in0=pages[1][:, cols], in1=share1[:, cols], op=ALU.add)
        nc.sync.dma_start(out=dealt_rows(out_0, 1).rearrange("p (h i) -> p h i", h=2), in_=y01[:, :, 1, :])
        nc.gpsimd.tensor_tensor(out=y23[:, :, 0, :], in0=by_chunks(pages[2][:]), in1=y23[:, :, 1, :], op=ALU.add)
        nc.sync.dma_start(out=by_chunks(dealt_rows(out_0, 2)), in_=y23[:, :, 0, :])

        y_woven = [tile("y_woven%d" % c, [P, CHUNK, PACK], BF16) for c in range(CHUNKS)]
        chunk_cols = [slice(CHUNK * c, CHUNK * (c + 1)) for c in range(CHUNKS)]
        for c in range(CHUNKS):
            cols = slice(CHUNK * (c % 2), CHUNK * (c % 2 + 1))
            nc.scalar.copy(out=y_woven[c][:, :, 0:2], in_=y01[:, c // 2, :, cols].rearrange("p e c -> p c e"))
        for chunks in (slice(0, 1), slice(1, 2), slice(2, 4)):
            nc.vector.scalar_tensor_tensor(
                out=y23[:, chunks, 1, :], in0=by_chunks(run_planes[3][:])[:, chunks], scalar=RUN_SHARE,
                in1=by_chunks(pages[3][:])[:, chunks], op0=ALU.mult, op1=ALU.add,
            )
        for chunks in (slice(0, 2), slice(2, 4)):
            nc.sync.dma_start(out=by_chunks(dealt_rows(out_0, 3))[:, chunks], in_=y23[:, chunks, 1, :])
        for engine_copy, c, cols in (
            (nc.scalar.copy, 0, slice(0, CHUNK)),
            (nc.vector.tensor_copy, 1, slice(0, CHUNK)),
            (nc.scalar.copy, 2, slice(0, CHUNK)),
            (nc.vector.tensor_copy, 3, slice(CHUNK // 2, CHUNK)),
            (nc.scalar.copy, 3, slice(0, CHUNK // 2)),
        ):
            engine_copy(out=y_woven[c][:, cols, 2:4], in_=y23[:, c, :, cols].rearrange("p e c -> p c e"))
        y_scale = tile("y_scale", [P, T], U8)
        words = out_1[0].rearrange("p c t -> p (c t)").bitcast(I32)
        for c in range(CHUNKS):
            y_codes = tile("y_codes%d" % c, [P, CHUNK], U32)
            nc.vector.quantize_mx(
                out=y_codes[:].bitcast(E4M3), scales=y_scale[:, chunk_cols[c]], in_=y_woven[c][:].rearrange("p c t -> p (c t)")
            )
            nc.sync.dma_start(out=words[:, chunk_cols[c]], in_=y_codes[:].bitcast(I32))
        scale_rows = out_2[0].bitcast(I32)
        for q in range(4):
            queue = nc.sync if q % 2 else nc.scalar
            queue.dma_start(out=scale_rows[4 * q : 4 * q + 4, :], in_=y_scale[32 * q : 32 * q + 4, :].bitcast(I32))
